import numpy as np
import ml_dtypes


def mxq(x, axis, fmt="e4m3"):
    dtype, down = {"e4m3": (ml_dtypes.float8_e4m3fn, 7), "e5m2": (ml_dtypes.float8_e5m2, 14)}[fmt]
    v = np.moveaxis(np.asarray(x, np.float32).astype(ml_dtypes.bfloat16).astype(np.float64), axis, -1)
    blocks = v.reshape(v.shape[:-1] + (-1, 32))
    amax = np.abs(blocks).max(-1, keepdims=True)
    byte = np.maximum(np.where(amax > 0, np.frexp(amax)[1] - 1 + 127, 0) - down, 1)
    scale = np.exp2(byte - 127.0)
    codes = (blocks / scale).astype(np.float32).astype(dtype).astype(np.float64)
    return np.moveaxis((codes * scale).reshape(v.shape), -1, axis)


WIDE = False


def mx_kscale(k):
    if not WIDE:
        return np.ones(k)
    levels = np.array([10, -10, 5, -5, 0])
    if k % 512:
        return np.exp2(np.random.permutation(np.resize(levels, k // 32))).repeat(32)
    a = np.empty((k // 512, 16))
    for p in range(k // 512):
        a[p, :8] = np.random.permutation(np.resize(levels, 8))
        for g in range(8):
            far = levels[np.abs(levels - a[p, g]) >= 10]
            a[p, g + 8] = far[np.random.randint(len(far))]
    return np.exp2(a.ravel()).repeat(32)


def f64(x):
    return np.asarray(x).astype(np.float64)


def striped(idx):
    return np.tile(idx.reshape(-1, 16).T, (8, 1)).astype(np.uint16)


def unstriped(offs):
    return offs[:16].T.reshape(-1).astype(np.int64)


def silu(v):
    return v / (1.0 + np.exp(-np.maximum(v, -700.0)))


K, T, E, C, H, N = 512, 2048, 8, 256, 512, 256


def by_expert(wq, xq):
    return np.concatenate([wq[e].T @ xq[:, e * C:(e + 1) * C] for e in range(E)], axis=1)


def setup_inputs():
    n = np.random.standard_normal
    s = mx_kscale(K)[:, None]
    u = mx_kscale(H)
    return {
        "xT": (n((K, T)) * s).astype(np.float32),
        "w1": (n((E, K, H)) / np.sqrt(K) / s[None]).astype(np.float32),
        "w3": (n((E, K, H)) / np.sqrt(K) / s[None] * u[None, None, :]).astype(np.float32),
        "w2": (n((E, H, N)) / np.sqrt(H) / u[None, :, None]).astype(np.float32),
        "gate": np.tile(np.random.uniform(0.2, 1.0, E * C), (N, 1)).astype(np.float32),
        "offs": striped(np.random.permutation(T)[:E * C]),
    }


def reference(xT, w1, w3, w2, gate, offs):
    idx = unstriped(offs)
    xq = mxq(f64(xT)[:, idx], 0, "e4m3")
    h = silu(by_expert(mxq(f64(w1), 1, "e4m3"), xq))
    h = h * by_expert(mxq(f64(w3), 1, "e4m3"), xq)
    y = by_expert(mxq(f64(w2), 1, "e4m3"), mxq(h, 0, "e4m3"))
    out = np.zeros((N, T))
    out[:, idx] = f64(gate) * y
    return out

@@ -1,0 +1,253 @@
+from contextlib import ExitStack
+
+import concourse.mybir as mybir
+
+K, T, E, C, H, N = 512, 2048, 8, 256, 512, 256
+FLOPS = 2 * E * C * (2 * K * H + H * N)
+BYTES = 4 * (K * T + 2 * E * K * H + E * H * N + E * C + N * T) + 2 * 128 * 128
+
+F32 = mybir.dt.float32
+BF16 = mybir.dt.bfloat16
+U32 = mybir.dt.uint32
+U16 = mybir.dt.uint16
+U8 = mybir.dt.uint8
+FP8X4 = mybir.dt.float8_e4m3fn_x4
+MULT = mybir.AluOpType.mult
+ADD = mybir.AluOpType.add
+SILU = mybir.ActivationFunctionType.Silu
+
+P = 128
+SCATTER_COPY = False
+W2ENG = ("G", "G")
+XENG = ("S", "V", "S", "SG")
+GCH = 1024
+PAIRS = E // 2
+
+
+def tile_routed_moe_kernel(tc, xT, w1, w3, w2, gate, offs, out):
+    nc = tc.nc
+    with ExitStack() as ctx:
+        lists = ctx.enter_context(tc.tile_pool(name="lists", bufs=1))
+        keep = ctx.enter_context(tc.tile_pool(name="keep", bufs=1))
+        raw = ctx.enter_context(tc.tile_pool(name="raw", bufs=8))
+        grp = ctx.enter_context(tc.tile_pool(name="grp", bufs=2))
+        cod = ctx.enter_context(tc.tile_pool(name="cod", bufs=2))
+        work = ctx.enter_context(tc.tile_pool(name="work", bufs=2))
+        psum = ctx.enter_context(tc.psum_pool(name="psum", bufs=3))
+
+        def cast(eng, dst, src):
+            if eng == "V":
+                nc.vector.tensor_copy(out=dst, in_=src)
+            elif eng == "S":
+                nc.scalar.copy(out=dst, in_=src)
+            else:
+                nc.gpsimd.tensor_scalar(out=dst, in0=src, scalar1=1.0, scalar2=0.0, op0=MULT, op1=ADD)
+
+        offsets = lists.tile([P, E * C // 16], U16, name="offsets")
+        nc.sync.dma_start(offsets[:], offs)
+
+        warm_in = keep.tile([P, 1], F32, name="warm_in")
+        warm_out = keep.tile([P, 1], F32, name="warm_out")
+        nc.vector.memset(warm_in[:], 0.0)
+        nc.scalar.activation(out=warm_out[:], in_=warm_in[:], func=SILU)
+
+        x_rows = xT.rearrange("(p j) n -> p j n", j=4)
+        xpair = [keep.tile([P, T, 2], BF16, name="xpair%d" % u) for u in range(2)]
+        for u in range(2):
+            for hf in range(2):
+                xr = raw.tile([P, 2, 1024], F32, tag="raw8", name="xraw%d%d" % (u, hf))
+                nc.sync.dma_start(xr[:], x_rows[:, 2 * u : 2 * u + 2, hf * 1024 : (hf + 1) * 1024])
+                engs = XENG[2 * u + hf]
+                w = 1024 // len(engs)
+                for k, eng in enumerate(engs):
+                    cast(
+                        eng,
+                        xpair[u][:, hf * 1024 + k * w : hf * 1024 + (k + 1) * w, :].rearrange("p (c i) e -> p c e i", i=4),
+                        xr[:, :, k * w : (k + 1) * w].rearrange("p e (c i) -> p c e i", i=4),
+                    )
+
+        gate_sb = keep.tile([P, E * C], F32, name="gate_sb")
+        win = [keep.tile([P, T], F32, name="win%d" % nb) for nb in range(2)]
+        xc = [keep.tile([P, GCH], U32, name="xc%d" % g, align_bytes=64) for g in range(E * C // GCH)]
+        xs = [keep.tile([P, GCH], U8, name="xs%d" % g, align_bytes=64) for g in range(E * C // GCH)]
+
+        def gather(g):
+            xg = work.tile([P, GCH, 4], BF16, tag="xg", name="xg%d" % g, align_bytes=64)
+            words = xg[:].rearrange("p n t -> p (n t)").bitcast(U32).rearrange("p (n u) -> p n u", u=2)
+            lst = offsets[:, g * (GCH // 16) : (g + 1) * (GCH // 16)]
+            for u in range(2):
+                window = xpair[u][:].rearrange("p n e -> p (n e)").bitcast(U32)
+                nc.vector.tensor_copy(out=words[:, :, u], in_=window.indirect(lst))
+            nc.vector.quantize_mx(out=xc[g][:].bitcast(FP8X4), scales=xs[g][:], in_=xg[:].rearrange("p n t -> p (n t)"))
+
+        rw = {}
+        g13 = {}
+        g2 = {}
+        c13 = {}
+        c2 = {}
+
+        def load(e):
+            r1 = raw.tile([P, 4, H], F32, tag="raw8", name="r1_%d" % e)
+            nc.sync.dma_start(r1[:], w1[e].rearrange("(p j) c -> p j c", j=4))
+            r3 = raw.tile([P, 4, H], F32, tag="raw8", name="r3_%d" % e)
+            nc.sync.dma_start(r3[:], w3[e].rearrange("(p j) c -> p j c", j=4))
+            r2 = raw.tile([P, 4, N], F32, tag="raw4", name="r2_%d" % e, bufs=4)
+            nc.sync.dma_start(r2[:], w2[e].rearrange("(p j) c -> p j c", j=4))
+            rw[e] = (r1, r3, r2)
+
+        def casts(e):
+            r1, r3, r2 = rw[e]
+            g = grp.tile([P, 8 * H], BF16, tag="wg", name="g13_%d" % e, align_bytes=64)
+            for k, r in enumerate((r1, r3)):
+                cast(
+                    "S",
+                    g[:, k * 4 * H : (k + 1) * 4 * H].rearrange("p (t m j) -> p m j t", t=4, j=4),
+                    r[:].rearrange("p j (m t) -> p m j t", t=4),
+                )
+            g13[e] = g
+            if e % 2 == 0:
+                g2[e // 2] = grp.tile([P, 8 * N], BF16, tag="wg2", name="g2_%d" % (e // 2), align_bytes=64)
+            o = (e % 2) * 4 * N
+            if W2ENG[e % 2] == "G":
+                cast("G", g2[e // 2][:, o : o + 4 * N].rearrange("p (c j) -> p c j", j=4), r2[:].rearrange("p j c -> p c j"))
+            else:
+                cast(
+                    W2ENG[e % 2],
+                    g2[e // 2][:, o : o + 4 * N].rearrange("p (c i j) -> p c j i", i=4, j=4),
+                    r2[:].rearrange("p j (c i) -> p c j i", i=4),
+                )
+
+        def quant_w(e):
+            c = cod.tile([P, 2 * H], U32, tag="c13", name="c13_%d" % e, align_bytes=64)
+            s = cod.tile([P, 2 * H], U8, tag="s13", name="s13_%d" % e, align_bytes=64)
+            nc.vector.quantize_mx(out=c[:].bitcast(FP8X4), scales=s[:], in_=g13[e][:])
+            c13[e] = (c, s)
+            if e % 2 == 1:
+                c = cod.tile([P, 2 * N], U32, tag="c2", name="c2_%d" % (e // 2), align_bytes=64)
+                s = cod.tile([P, 2 * N], U8, tag="s2", name="s2_%d" % (e // 2), align_bytes=64)
+                nc.vector.quantize_mx(out=c[:].bitcast(FP8X4), scales=s[:], in_=g2[e // 2][:])
+                c2[e // 2] = (c, s)
+
+        hbt = {}
+        yps = {}
+        ysb = {}
+
+        def first_layer(k, m, ps):
+            e = k // 2
+            c, s = c13[e]
+            g, o = (k * 128) // GCH, (k * 128) % GCH
+            for t in range(4):
+                col = m * H + 128 * t
+                nc.tensor.matmul_mx(
+                    out=ps[:, t, :],
+                    lhsT=c[:, col : col + 128].bitcast(FP8X4),
+                    lhsT_scale=s[:, col : col + 128],
+                    rhs=xc[g][:, o : o + 128].bitcast(FP8X4),
+                    rhs_scale=xs[g][:, o : o + 128],
+                    start=True,
+                    stop=True,
+                )
+
+        sat = {}
+        bps = {}
+
+        def mma(k):
+            a_ps = psum.tile([P, 4, 128], F32, tag="a", name="a%d" % k, bufs=4)
+            first_layer(k, 0, a_ps)
+            sa = work.tile([P, 128, 4], F32, tag="sa", name="sa%d" % k, bufs=6)
+            nc.scalar.activation(out=sa[:], in_=a_ps[:].rearrange("p t c -> p c t"), func=SILU)
+            sat[k] = sa
+
+        def mmb(k):
+            b_ps = psum.tile([P, 4, 128], F32, tag="by", name="b%d" % k, bufs=2)
+            first_layer(k, 1, b_ps)
+            bps[k] = b_ps
+
+        def mult(k):
+            e, hf = k // 2, k % 2
+            if hf == 0:
+                hbt[e] = work.tile([P, C, 4], BF16, tag="hb", name="hb%d" % e, align_bytes=64)
+            nc.vector.tensor_tensor(
+                out=hbt[e][:, hf * 128 : hf * 128 + 128, :], in0=sat[k][:], in1=bps[k][:].rearrange("p t c -> p c t"), op=MULT
+            )
+
+        hcs = {}
+
+        def qh(e):
+            hc = work.tile([P, C], U32, tag="hc", name="hc%d" % e, align_bytes=64)
+            hs = work.tile([P, C], U8, tag="hs", name="hs%d" % e, align_bytes=64)
+            nc.vector.quantize_mx(out=hc[:].bitcast(FP8X4), scales=hs[:], in_=hbt[e][:].rearrange("p c t -> p (c t)"))
+            hcs[e] = (hc, hs)
+
+        def mm2(e):
+            c, s = c2[e // 2]
+            hc, hs = hcs[e]
+            y_ps = psum.tile([P, 2, C], F32, tag="by", name="y%d" % e, bufs=2)
+            for nb in range(2):
+                col = (e % 2) * N + nb * 128
+                nc.tensor.matmul_mx(
+                    out=y_ps[:, nb, :],
+                    lhsT=c[:, col : col + 128].bitcast(FP8X4),
+                    lhsT_scale=s[:, col : col + 128],
+                    rhs=hc[:].bitcast(FP8X4),
+                    rhs_scale=hs[:],
+                    start=True,
+                    stop=True,
+                )
+            yps[e] = y_ps
+
+        def evac(e):
+            y = work.tile([P, 2, C], F32, tag="ysb", name="ysb%d" % e, bufs=3)
+            if SCATTER_COPY:
+                for nb in range(2):
+                    nc.vector.tensor_tensor(out=y[:, nb, :], in0=yps[e][:, nb, :], in1=gate_sb[:, e * C : (e + 1) * C], op=MULT)
+            else:
+                nc.scalar.copy(out=y[:], in_=yps[e][:])
+            ysb[e] = y
+
+        def scatter(e, nb):
+            lst = offsets[:, e * (C // 16) : (e + 1) * (C // 16)]
+            if SCATTER_COPY:
+                nc.vector.tensor_copy(out=win[nb][:].indirect(lst), in_=ysb[e][:, nb, :])
+            else:
+                nc.vector.tensor_tensor(
+                    out=win[nb][:].indirect(lst), in0=ysb[e][:, nb, :], in1=gate_sb[:, e * C : (e + 1) * C], op=MULT
+                )
+
+        nc.sync.dma_start(gate_sb[:], gate[0:P, :])
+        for e in range(4):
+            load(e)
+        gather(0)
+        gather(1)
+        for e in range(2):
+            casts(e)
+            quant_w(e)
+        mma(0)
+        mma(1)
+        for e in range(E):
+            if e + 1 < E:
+                mma(2 * e + 2)
+                mma(2 * e + 3)
+            mmb(2 * e)
+            mmb(2 * e + 1)
+            mult(2 * e)
+            if e >= 1:
+                mm2(e - 1)
+                evac(e - 1)
+            if e >= 2:
+                scatter(e - 2, 0)
+                scatter(e - 2, 1)
+            mult(2 * e + 1)
+            qh(e)
+            if e + 2 < E:
+                casts(e + 2)
+                quant_w(e + 2)
+                if e + 4 < E:
+                    load(e + 4)
+        mm2(E - 1)
+        evac(E - 1)
+        scatter(E - 2, 0)
+        scatter(E - 2, 1)
+        for nb in range(2):
+            scatter(E - 1, nb)
+            nc.sync.dma_start(out[nb * P : (nb + 1) * P, :], win[nb][:])

@@ -159,7 +159,7 @@ def tile_routed_moe_kernel(tc, xT, w1, w3, w2, gate, offs, out):
             sat[k] = sa
 
         def mmb(k):
-            b_ps = psum.tile([P, 4, 128], F32, tag="by", name="b%d" % k, bufs=2)
+            b_ps = psum.tile([P, 4, 128], F32, tag="by", name="b%d" % k, bufs=4)
             first_layer(k, 1, b_ps)
             bps[k] = b_ps
 
@@ -182,7 +182,7 @@ def tile_routed_moe_kernel(tc, xT, w1, w3, w2, gate, offs, out):
         def mm2(e):
             c, s = c2[e // 2]
             hc, hs = hcs[e]
-            y_ps = psum.tile([P, 2, C], F32, tag="by", name="y%d" % e, bufs=2)
+            y_ps = psum.tile([P, 2, C], F32, tag="by", name="y%d" % e, bufs=4)
             for nb in range(2):
                 col = (e % 2) * N + nb * 128
                 nc.tensor.matmul_mx(

@@ -22,6 +22,7 @@ W2ENG = ("G", "G")
 XENG = ("S", "V", "S", "SG")
 GCH = 1024
 PAIRS = E // 2
+LINK_SLOT = 4 * H * 4 + 64 + 2 * C * 4 + 64 + 2048
 
 
 def tile_routed_moe_kernel(tc, xT, w1, w3, w2, gate, offs, out):
@@ -29,7 +30,8 @@ def tile_routed_moe_kernel(tc, xT, w1, w3, w2, gate, offs, out):
     with ExitStack() as ctx:
         lists = ctx.enter_context(tc.tile_pool(name="lists", bufs=1))
         keep = ctx.enter_context(tc.tile_pool(name="keep", bufs=1))
-        raw = ctx.enter_context(tc.tile_pool(name="raw", bufs=8))
+        raw = ctx.enter_context(tc.tile_pool(name="raw", bufs=4))
+        link = ctx.enter_context(tc.tile_pool(name="link", bufs=1))
         grp = ctx.enter_context(tc.tile_pool(name="grp", bufs=2))
         cod = ctx.enter_context(tc.tile_pool(name="cod", bufs=2))
         work = ctx.enter_context(tc.tile_pool(name="work", bufs=2))
@@ -87,10 +89,12 @@ def tile_routed_moe_kernel(tc, xT, w1, w3, w2, gate, offs, out):
         c2 = {}
 
         def load(e):
-            r1 = raw.tile([P, 4, H], F32, tag="raw8", name="r1_%d" % e)
-            nc.sync.dma_start(r1[:], w1[e].rearrange("(p j) c -> p j c", j=4))
-            r3 = raw.tile([P, 4, H], F32, tag="raw8", name="r3_%d" % e)
-            nc.sync.dma_start(r3[:], w3[e].rearrange("(p j) c -> p j c", j=4))
+            r1t = raw.tile([P, 4, H], F32, tag="raw8", name="r1_%d" % e)
+            r1 = r1t[:]
+            nc.sync.dma_start(r1, w1[e].rearrange("(p j) c -> p j c", j=4))
+            r3t = link.tile([P, 4 * H + 16], F32, name="r3_%d" % e, align_bytes=64, offset=(e % 4) * LINK_SLOT)
+            r3 = r3t[:, 0 : 4 * H].rearrange("p (j c) -> p j c", j=4)
+            nc.sync.dma_start(r3, w3[e].rearrange("(p j) c -> p j c", j=4))
             r2 = raw.tile([P, 4, N], F32, tag="raw4", name="r2_%d" % e, bufs=4)
             nc.sync.dma_start(r2[:], w2[e].rearrange("(p j) c -> p j c", j=4))
             rw[e] = (r1, r3, r2)
@@ -102,7 +106,7 @@ def tile_routed_moe_kernel(tc, xT, w1, w3, w2, gate, offs, out):
                 cast(
                     "S",
                     g[:, k * 4 * H : (k + 1) * 4 * H].rearrange("p (t m j) -> p m j t", t=4, j=4),
-                    r[:].rearrange("p j (m t) -> p m j t", t=4),
+                    r.rearrange("p j (m t) -> p m j t", t=4),
                 )
             g13[e] = g
             if e % 2 == 0:
@@ -154,8 +158,13 @@ def tile_routed_moe_kernel(tc, xT, w1, w3, w2, gate, offs, out):
         def mma(k):
             a_ps = psum.tile([P, 4, 128], F32, tag="a", name="a%d" % k, bufs=4)
             first_layer(k, 0, a_ps)
-            sa = work.tile([P, 128, 4], F32, tag="sa", name="sa%d" % k, bufs=6)
-            nc.scalar.activation(out=sa[:], in_=a_ps[:].rearrange("p t c -> p c t"), func=SILU)
+            if k == 2 * (E - 1):
+                st = link.tile([P, 16 + 512], F32, name="sa%d" % k, align_bytes=64, offset=(E % 4) * LINK_SLOT + 4 * H * 4 + 64 + 2 * C * 4)
+                sa = st[:, 16:].rearrange("p (c t) -> p c t", t=4)
+            else:
+                st = work.tile([P, 128, 4], F32, tag="sa", name="sa%d" % k, bufs=6)
+                sa = st[:]
+            nc.scalar.activation(out=sa, in_=a_ps[:].rearrange("p t c -> p c t"), func=SILU)
             sat[k] = sa
 
         def mmb(k):
@@ -168,7 +177,7 @@ def tile_routed_moe_kernel(tc, xT, w1, w3, w2, gate, offs, out):
             if hf == 0:
                 hbt[e] = work.tile([P, C, 4], BF16, tag="hb", name="hb%d" % e, align_bytes=64)
             nc.vector.tensor_tensor(
-                out=hbt[e][:, hf * 128 : hf * 128 + 128, :], in0=sat[k][:], in1=bps[k][:].rearrange("p t c -> p c t"), op=MULT
+                out=hbt[e][:, hf * 128 : hf * 128 + 128, :], in0=sat[k], in1=bps[k][:].rearrange("p t c -> p c t"), op=MULT
             )
 
         hcs = {}
@@ -197,12 +206,11 @@ def tile_routed_moe_kernel(tc, xT, w1, w3, w2, gate, offs, out):
             yps[e] = y_ps
 
         def evac(e):
-            y = work.tile([P, 2, C], F32, tag="ysb", name="ysb%d" % e, bufs=3)
-            if SCATTER_COPY:
-                for nb in range(2):
-                    nc.vector.tensor_tensor(out=y[:, nb, :], in0=yps[e][:, nb, :], in1=gate_sb[:, e * C : (e + 1) * C], op=MULT)
-            else:
-                nc.scalar.copy(out=y[:], in_=yps[e][:])
+            yt = link.tile(
+                [P, 16 + 2 * C + (16 if e == E - 2 else 0)], F32, name="ysb%d" % e, align_bytes=64, offset=((e + 2) % 4) * LINK_SLOT + 4 * H * 4
+            )
+            y = yt[:, 16 : 16 + 2 * C].rearrange("p (n c) -> p n c", n=2)
+            nc.scalar.copy(out=y, in_=yps[e][:])
             ysb[e] = y
 
         def scatter(e, nb):

@@ -71,7 +71,11 @@ def tile_routed_moe_kernel(tc, xT, w1, w3, w2, gate, offs, out):
         gate_sb = keep.tile([P, E * C], F32, name="gate_sb")
         win = [keep.tile([P, T], F32, name="win%d" % nb) for nb in range(2)]
         xc = [keep.tile([P, GCH], U32, name="xc%d" % g, align_bytes=64) for g in range(E * C // GCH)]
-        xs = [keep.tile([P, GCH], U8, name="xs%d" % g, align_bytes=64) for g in range(E * C // GCH)]
+        xs0 = keep.tile([P, GCH], U8, name="xs0", align_bytes=64)
+        xs1 = link.tile([P, 64 + GCH], U8, name="xs1", align_bytes=64, offset=4 * LINK_SLOT + 8 * H * 2)
+        xs = [xs0[:], xs1[:, 64:]]
+
+        xgt = {}
 
         def gather(g):
             xg = work.tile([P, GCH, 4], BF16, tag="xg", name="xg%d" % g, align_bytes=64)
@@ -80,7 +84,10 @@ def tile_routed_moe_kernel(tc, xT, w1, w3, w2, gate, offs, out):
             for u in range(2):
                 window = xpair[u][:].rearrange("p n e -> p (n e)").bitcast(U32)
                 nc.vector.tensor_copy(out=words[:, :, u], in_=window.indirect(lst))
-            nc.vector.quantize_mx(out=xc[g][:].bitcast(FP8X4), scales=xs[g][:], in_=xg[:].rearrange("p n t -> p (n t)"))
+            xgt[g] = xg
+
+        def quant_x(g):
+            nc.vector.quantize_mx(out=xc[g][:].bitcast(FP8X4), scales=xs[g], in_=xgt[g][:].rearrange("p n t -> p (n t)"))
 
         rw = {}
         g13 = {}
@@ -101,7 +108,14 @@ def tile_routed_moe_kernel(tc, xT, w1, w3, w2, gate, offs, out):
 
         def casts(e):
             r1, r3, r2 = rw[e]
-            g = grp.tile([P, 8 * H], BF16, tag="wg", name="g13_%d" % e, align_bytes=64)
+            gt = link.tile(
+                [P, 8 * H + (32 if e == 0 else 0)],
+                BF16,
+                name="g13_%d" % e,
+                align_bytes=64,
+                offset=4 * LINK_SLOT + (e % 2) * (8 * H * 2 + 64 + GCH),
+            )
+            g = gt[:, 0 : 8 * H]
             for k, r in enumerate((r1, r3)):
                 cast(
                     "S",
@@ -124,7 +138,7 @@ def tile_routed_moe_kernel(tc, xT, w1, w3, w2, gate, offs, out):
         def quant_w(e):
             c = cod.tile([P, 2 * H], U32, tag="c13", name="c13_%d" % e, align_bytes=64)
             s = cod.tile([P, 2 * H], U8, tag="s13", name="s13_%d" % e, align_bytes=64)
-            nc.vector.quantize_mx(out=c[:].bitcast(FP8X4), scales=s[:], in_=g13[e][:])
+            nc.vector.quantize_mx(out=c[:].bitcast(FP8X4), scales=s[:], in_=g13[e])
             c13[e] = (c, s)
             if e % 2 == 1:
                 c = cod.tile([P, 2 * N], U32, tag="c2", name="c2_%d" % (e // 2), align_bytes=64)
@@ -226,10 +240,13 @@ def tile_routed_moe_kernel(tc, xT, w1, w3, w2, gate, offs, out):
         for e in range(4):
             load(e)
         gather(0)
+        quant_x(0)
         gather(1)
-        for e in range(2):
-            casts(e)
-            quant_w(e)
+        casts(0)
+        quant_w(0)
+        quant_x(1)
+        casts(1)
+        quant_w(1)
         mma(0)
         mma(1)
         for e in range(E):

@@ -198,8 +198,9 @@ def tile_routed_moe_kernel(tc, xT, w1, w3, w2, gate, offs, out):
 
         def qh(e):
             hc = work.tile([P, C], U32, tag="hc", name="hc%d" % e, align_bytes=64)
-            hs = work.tile([P, C], U8, tag="hs", name="hs%d" % e, align_bytes=64)
-            nc.vector.quantize_mx(out=hc[:].bitcast(FP8X4), scales=hs[:], in_=hbt[e][:].rearrange("p c t -> p (c t)"))
+            hst = link.tile([P, 64 + C], U8, name="hs%d" % e, align_bytes=64, offset=(e % 4) * LINK_SLOT + 4 * H * 4 + 64 + 2 * C * 4)
+            hs = hst[:, 64:]
+            nc.vector.quantize_mx(out=hc[:].bitcast(FP8X4), scales=hs, in_=hbt[e][:].rearrange("p c t -> p (c t)"))
             hcs[e] = (hc, hs)
 
         def mm2(e):
@@ -213,7 +214,7 @@ def tile_routed_moe_kernel(tc, xT, w1, w3, w2, gate, offs, out):
                     lhsT=c[:, col : col + 128].bitcast(FP8X4),
                     lhsT_scale=s[:, col : col + 128],
                     rhs=hc[:].bitcast(FP8X4),
-                    rhs_scale=hs[:],
+                    rhs_scale=hs,
                     start=True,
                     stop=True,
                 )
@@ -221,7 +222,7 @@ def tile_routed_moe_kernel(tc, xT, w1, w3, w2, gate, offs, out):
 
         def evac(e):
             yt = link.tile(
-                [P, 16 + 2 * C + (16 if e == E - 2 else 0)], F32, name="ysb%d" % e, align_bytes=64, offset=((e + 2) % 4) * LINK_SLOT + 4 * H * 4
+                [P, 16 + 2 * C + 16], F32, name="ysb%d" % e, align_bytes=64, offset=((e + 2) % 4) * LINK_SLOT + 4 * H * 4
             )
             y = yt[:, 16 : 16 + 2 * C].rearrange("p (n c) -> p n c", n=2)
             nc.scalar.copy(out=y, in_=yps[e][:])

@@ -17,12 +17,23 @@ ADD = mybir.AluOpType.add
 SILU = mybir.ActivationFunctionType.Silu
 
 P = 128
-SCATTER_COPY = False
-W2ENG = ("G", "G")
-XENG = ("S", "V", "S", "SG")
 GCH = 1024
+NCH = E * C // GCH
+XP = ((0, 0, 1024, "S"), (0, 1024, 512, "V"), (0, 1536, 512, "V"), (1, 0, 1024, "S"), (1, 1024, 512, "G"), (1, 1536, 512, "SG"))
+LOADS = "a0 b0 a1 c0 g0 b1 a2 c1 g1 b2 a3 c2 g2 b3"
+LATE = "a0 c1 g1 b0"
+W2SPLIT = False
+GATE = 8
+CASTENG = {}
+ORDER = "N"
+W2LAG = 0
+YTIE = True
+YFREE = ()
+NEXP = 8
 PAIRS = E // 2
 LINK_SLOT = 4 * H * 4 + 64 + 2 * C * 4 + 64 + 2048
+GT_SIZE = GCH + 64 + 8 * H * 2 + 64 + 4 * C * 2
+HBTIE = ()
 
 
 def tile_routed_moe_kernel(tc, xT, w1, w3, w2, gate, offs, out):
@@ -55,25 +66,28 @@ def tile_routed_moe_kernel(tc, xT, w1, w3, w2, gate, offs, out):
 
         x_rows = xT.rearrange("(p j) n -> p j n", j=4)
         xpair = [keep.tile([P, T, 2], BF16, name="xpair%d" % u) for u in range(2)]
-        for u in range(2):
-            for hf in range(2):
-                xr = raw.tile([P, 2, 1024], F32, tag="raw8", name="xraw%d%d" % (u, hf))
-                nc.sync.dma_start(xr[:], x_rows[:, 2 * u : 2 * u + 2, hf * 1024 : (hf + 1) * 1024])
-                engs = XENG[2 * u + hf]
-                w = 1024 // len(engs)
-                for k, eng in enumerate(engs):
-                    cast(
-                        eng,
-                        xpair[u][:, hf * 1024 + k * w : hf * 1024 + (k + 1) * w, :].rearrange("p (c i) e -> p c e i", i=4),
-                        xr[:, :, k * w : (k + 1) * w].rearrange("p e (c i) -> p c e i", i=4),
-                    )
+        for u, t0, n, engs in XP:
+            xr = raw.tile([P, 2, n], F32, tag="raw8", name="xraw%d_%d" % (u, t0))
+            nc.sync.dma_start(xr[:], x_rows[:, 2 * u : 2 * u + 2, t0 : t0 + n])
+            w = n // len(engs)
+            for k, eng in enumerate(engs):
+                cast(
+                    eng,
+                    xpair[u][:, t0 + k * w : t0 + (k + 1) * w, :].rearrange("p (c i) e -> p c e i", i=4),
+                    xr[:, :, k * w : (k + 1) * w].rearrange("p e (c i) -> p c e i", i=4),
+                )
 
         gate_sb = keep.tile([P, E * C], F32, name="gate_sb")
         win = [keep.tile([P, T], F32, name="win%d" % nb) for nb in range(2)]
-        xc = [keep.tile([P, GCH], U32, name="xc%d" % g, align_bytes=64) for g in range(E * C // GCH)]
-        xs0 = keep.tile([P, GCH], U8, name="xs0", align_bytes=64)
-        xs1 = link.tile([P, 64 + GCH], U8, name="xs1", align_bytes=64, offset=4 * LINK_SLOT + 8 * H * 2)
-        xs = [xs0[:], xs1[:, 64:]]
+        xc = [keep.tile([P, GCH], U32, name="xc%d" % g, align_bytes=64) for g in range(NCH)]
+        xs = []
+        for g in range(NCH):
+            if g == NCH - 1:
+                xs1 = link.tile([P, GCH + 64], U8, name="xs1", align_bytes=64, offset=4 * LINK_SLOT)
+                xs.append(xs1[:, 0:GCH])
+            else:
+                xs0 = keep.tile([P, GCH], U8, name="xs%d" % g, align_bytes=64)
+                xs.append(xs0[:])
 
         xgt = {}
 
@@ -89,58 +103,78 @@ def tile_routed_moe_kernel(tc, xT, w1, w3, w2, gate, offs, out):
         def quant_x(g):
             nc.vector.quantize_mx(out=xc[g][:].bitcast(FP8X4), scales=xs[g], in_=xgt[g][:].rearrange("p n t -> p (n t)"))
 
-        rw = {}
+        rw13 = {}
+        rw2 = {}
         g13 = {}
         g2 = {}
         c13 = {}
         c2 = {}
 
-        def load(e):
+        def loadg(k):
+            n = E * C // GATE
+            nc.sync.dma_start(gate_sb[:, k * n : (k + 1) * n], gate[0:P, k * n : (k + 1) * n])
+
+        def loada(e):
             r1t = raw.tile([P, 4, H], F32, tag="raw8", name="r1_%d" % e)
-            r1 = r1t[:]
-            nc.sync.dma_start(r1, w1[e].rearrange("(p j) c -> p j c", j=4))
+            nc.sync.dma_start(r1t[:], w1[e].rearrange("(p j) c -> p j c", j=4))
+            rw13[e] = [r1t[:], None]
+
+        def loadb(e):
             r3t = link.tile([P, 4 * H + 16], F32, name="r3_%d" % e, align_bytes=64, offset=(e % 4) * LINK_SLOT)
             r3 = r3t[:, 0 : 4 * H].rearrange("p (j c) -> p j c", j=4)
             nc.sync.dma_start(r3, w3[e].rearrange("(p j) c -> p j c", j=4))
+            rw13[e][1] = r3
+
+        def load2(e):
             r2 = raw.tile([P, 4, N], F32, tag="raw4", name="r2_%d" % e, bufs=4)
             nc.sync.dma_start(r2[:], w2[e].rearrange("(p j) c -> p j c", j=4))
-            rw[e] = (r1, r3, r2)
+            rw2[e] = r2
 
-        def casts(e):
-            r1, r3, r2 = rw[e]
+        def casts13(e):
+            head = 32 if e == 0 else 0
+            tail = 32 if e - 1 in HBTIE else 0
             gt = link.tile(
-                [P, 8 * H + (32 if e == 0 else 0)],
+                [P, head + 8 * H + tail],
                 BF16,
                 name="g13_%d" % e,
                 align_bytes=64,
-                offset=4 * LINK_SLOT + (e % 2) * (8 * H * 2 + 64 + GCH),
+                offset=4 * LINK_SLOT + (e % 2) * GT_SIZE + GCH + 64 - 2 * head,
             )
-            g = gt[:, 0 : 8 * H]
-            for k, r in enumerate((r1, r3)):
+            g = gt[:, head : head + 8 * H]
+            for k in range(2):
+                r = rw13[e][k]
                 cast(
-                    "S",
+                    CASTENG.get((e, k), "S"),
                     g[:, k * 4 * H : (k + 1) * 4 * H].rearrange("p (t m j) -> p m j t", t=4, j=4),
                     r.rearrange("p j (m t) -> p m j t", t=4),
                 )
             g13[e] = g
+
+        def casts2(e):
+            r2 = rw2[e]
             if e % 2 == 0:
                 g2[e // 2] = grp.tile([P, 8 * N], BF16, tag="wg2", name="g2_%d" % (e // 2), align_bytes=64)
             o = (e % 2) * 4 * N
-            if W2ENG[e % 2] == "G":
-                cast("G", g2[e // 2][:, o : o + 4 * N].rearrange("p (c j) -> p c j", j=4), r2[:].rearrange("p j c -> p c j"))
-            else:
-                cast(
-                    W2ENG[e % 2],
-                    g2[e // 2][:, o : o + 4 * N].rearrange("p (c i j) -> p c j i", i=4, j=4),
-                    r2[:].rearrange("p j (c i) -> p c j i", i=4),
-                )
+            cast("G", g2[e // 2][:, o : o + 4 * N].rearrange("p (c j) -> p c j", j=4), r2[:].rearrange("p j c -> p c j"))
 
         def quant_w(e):
             c = cod.tile([P, 2 * H], U32, tag="c13", name="c13_%d" % e, align_bytes=64)
             s = cod.tile([P, 2 * H], U8, tag="s13", name="s13_%d" % e, align_bytes=64)
             nc.vector.quantize_mx(out=c[:].bitcast(FP8X4), scales=s[:], in_=g13[e])
             c13[e] = (c, s)
-            if e % 2 == 1:
+
+        def quant_w2(e):
+            if W2SPLIT:
+                if e % 2 == 0:
+                    c = cod.tile([P, 2 * N], U32, tag="c2", name="c2_%d" % (e // 2), align_bytes=64)
+                    s = cod.tile([P, 2 * N], U8, tag="s2", name="s2_%d" % (e // 2), align_bytes=64)
+                    c2[e // 2] = (c, s)
+                c, s = c2[e // 2]
+                o = (e % 2) * N
+                nc.vector.quantize_mx(
+                    out=c[:, o : o + N].bitcast(FP8X4), scales=s[:, o : o + N], in_=g2[e // 2][:, 4 * o : 4 * o + 4 * N]
+                )
+            elif e % 2 == 1:
                 c = cod.tile([P, 2 * N], U32, tag="c2", name="c2_%d" % (e // 2), align_bytes=64)
                 s = cod.tile([P, 2 * N], U8, tag="s2", name="s2_%d" % (e // 2), align_bytes=64)
                 nc.vector.quantize_mx(out=c[:].bitcast(FP8X4), scales=s[:], in_=g2[e // 2][:])
@@ -172,7 +206,7 @@ def tile_routed_moe_kernel(tc, xT, w1, w3, w2, gate, offs, out):
         def mma(k):
             a_ps = psum.tile([P, 4, 128], F32, tag="a", name="a%d" % k, bufs=4)
             first_layer(k, 0, a_ps)
-            if k == 2 * (E - 1):
+            if k == 2 * (E - 1) and YTIE:
                 st = link.tile([P, 16 + 512], F32, name="sa%d" % k, align_bytes=64, offset=(E % 4) * LINK_SLOT + 4 * H * 4 + 64 + 2 * C * 4)
                 sa = st[:, 16:].rearrange("p (c t) -> p c t", t=4)
             else:
@@ -189,7 +223,14 @@ def tile_routed_moe_kernel(tc, xT, w1, w3, w2, gate, offs, out):
         def mult(k):
             e, hf = k // 2, k % 2
             if hf == 0:
-                hbt[e] = work.tile([P, C, 4], BF16, tag="hb", name="hb%d" % e, align_bytes=64)
+                if HBTIE:
+                    pad = 32 if e in HBTIE else 0
+                    ht = link.tile(
+                        [P, pad + 4 * C], BF16, name="hb%d" % e, align_bytes=64, offset=4 * LINK_SLOT + ((e + 1) % 2) * GT_SIZE + GCH + 128 + 8 * H * 2 - 2 * pad
+                    )
+                    hbt[e] = ht[:, pad:].rearrange("p (c t) -> p c t", t=4)
+                else:
+                    hbt[e] = work.tile([P, C, 4], BF16, tag="hb", name="hb%d" % e, align_bytes=64)[:]
             nc.vector.tensor_tensor(
                 out=hbt[e][:, hf * 128 : hf * 128 + 128, :], in0=sat[k], in1=bps[k][:].rearrange("p t c -> p c t"), op=MULT
             )
@@ -198,9 +239,12 @@ def tile_routed_moe_kernel(tc, xT, w1, w3, w2, gate, offs, out):
 
         def qh(e):
             hc = work.tile([P, C], U32, tag="hc", name="hc%d" % e, align_bytes=64)
-            hst = link.tile([P, 64 + C], U8, name="hs%d" % e, align_bytes=64, offset=(e % 4) * LINK_SLOT + 4 * H * 4 + 64 + 2 * C * 4)
+            if YTIE:
+                hst = link.tile([P, 64 + C], U8, name="hs%d" % e, align_bytes=64, offset=(e % 4) * LINK_SLOT + 4 * H * 4 + 64 + 2 * C * 4)
+            else:
+                hst = work.tile([P, 64 + C], U8, tag="hs", name="hs%d" % e, align_bytes=64)
             hs = hst[:, 64:]
-            nc.vector.quantize_mx(out=hc[:].bitcast(FP8X4), scales=hs, in_=hbt[e][:].rearrange("p c t -> p (c t)"))
+            nc.vector.quantize_mx(out=hc[:].bitcast(FP8X4), scales=hs, in_=hbt[e].rearrange("p c t -> p (c t)"))
             hcs[e] = (hc, hs)
 
         def mm2(e):
@@ -221,37 +265,62 @@ def tile_routed_moe_kernel(tc, xT, w1, w3, w2, gate, offs, out):
             yps[e] = y_ps
 
         def evac(e):
-            yt = link.tile(
-                [P, 16 + 2 * C + 16], F32, name="ysb%d" % e, align_bytes=64, offset=((e + 2) % 4) * LINK_SLOT + 4 * H * 4
-            )
+            if e in YFREE:
+                yt = keep.tile([P, 16 + 2 * C + 16], F32, name="ysb%d" % e, align_bytes=64)
+            else:
+                yt = link.tile(
+                    [P, 16 + 2 * C + 16], F32, name="ysb%d" % e, align_bytes=64, offset=((e + 2) % 4) * LINK_SLOT + 4 * H * 4
+                )
             y = yt[:, 16 : 16 + 2 * C].rearrange("p (n c) -> p n c", n=2)
             nc.scalar.copy(out=y, in_=yps[e][:])
             ysb[e] = y
 
         def scatter(e, nb):
             lst = offsets[:, e * (C // 16) : (e + 1) * (C // 16)]
-            if SCATTER_COPY:
-                nc.vector.tensor_copy(out=win[nb][:].indirect(lst), in_=ysb[e][:, nb, :])
-            else:
-                nc.vector.tensor_tensor(
-                    out=win[nb][:].indirect(lst), in0=ysb[e][:, nb, :], in1=gate_sb[:, e * C : (e + 1) * C], op=MULT
-                )
+            nc.vector.tensor_tensor(
+                out=win[nb][:].indirect(lst), in0=ysb[e][:, nb, :], in1=gate_sb[:, e * C : (e + 1) * C], op=MULT
+            )
 
-        nc.sync.dma_start(gate_sb[:], gate[0:P, :])
-        for e in range(4):
-            load(e)
+        loaders = {"a": loada, "b": loadb, "c": load2, "g": loadg}
+        loaded = set()
+
+        def load(kind, n):
+            if kind != "g" or n < GATE:
+                loaders[kind](n)
+            loaded.add((kind, n))
+
+        if NEXP < E:
+            for nb in range(2):
+                nc.vector.memset(win[nb][:], 0.0)
+        for tok in LOADS.split(" "):
+            if int(tok[1:]) < NEXP:
+                load(tok[0], int(tok[1:]))
         gather(0)
         quant_x(0)
         gather(1)
-        casts(0)
+        if NCH == 4:
+            quant_x(1)
+            gather(2)
+            quant_x(2)
+            gather(3)
+        casts13(0)
+        casts2(0)
         quant_w(0)
-        quant_x(1)
-        casts(1)
-        quant_w(1)
+        quant_w2(0)
+        quant_x(NCH - 1)
+        if NEXP > 1:
+            casts13(1)
+            casts2(1)
+            quant_w(1)
+            quant_w2(1)
         mma(0)
         mma(1)
-        for e in range(E):
-            if e + 1 < E:
+        for e in range(NEXP):
+            for tok in LATE.split(" "):
+                n = e + 4 - int(tok[1:])
+                if n < NEXP and (tok[0], n) not in loaded:
+                    load(tok[0], n)
+            if e + 1 < NEXP:
                 mma(2 * e + 2)
                 mma(2 * e + 3)
             mmb(2 * e)
@@ -265,15 +334,16 @@ def tile_routed_moe_kernel(tc, xT, w1, w3, w2, gate, offs, out):
                 scatter(e - 2, 1)
             mult(2 * e + 1)
             qh(e)
-            if e + 2 < E:
-                casts(e + 2)
+            if e + 2 < NEXP:
+                casts13(e + 2)
+                casts2(e + 2)
                 quant_w(e + 2)
-                if e + 4 < E:
-                    load(e + 4)
-        mm2(E - 1)
-        evac(E - 1)
-        scatter(E - 2, 0)
-        scatter(E - 2, 1)
+                quant_w2(e + 2)
+        mm2(NEXP - 1)
+        evac(NEXP - 1)
+        if NEXP > 1:
+            scatter(NEXP - 2, 0)
+            scatter(NEXP - 2, 1)
         for nb in range(2):
-            scatter(E - 1, nb)
+            scatter(NEXP - 1, nb)
             nc.sync.dma_start(out[nb * P : (nb + 1) * P, :], win[nb][:])

@@ -18,22 +18,32 @@ SILU = mybir.ActivationFunctionType.Silu
 
 P = 128
 GCH = 1024
+GPLAIN = ()
+GPIECES = 4
 NCH = E * C // GCH
-XP = ((0, 0, 1024, "S"), (0, 1024, 512, "V"), (0, 1536, 512, "V"), (1, 0, 1024, "S"), (1, 1024, 512, "G"), (1, 1536, 512, "SG"))
-LOADS = "a0 b0 a1 c0 g0 b1 a2 c1 g1 b2 a3 c2 g2 b3"
-LATE = "a0 c1 g1 b0"
-W2SPLIT = False
+XP = ((0, 0, 1024, "S"), (0, 1024, 512, "V"), (0, 1536, 256, "V"), (0, 1792, 256, "V"), (1, 0, 1024, "S"), (1, 1024, 512, "G"), (1, 1536, 512, "SG"))
+SEQ = "x0 x1 x2 x3 o0 x4 x5 x6 a0 b0 a1 c0 g0 b1 a2 c1 g1 b2 a3 c2 g2 b3 a4 c3 g3 b4 a5 c4 g4 b5 a6 c5 g5 b6 a7 c6 g6 b7 c7 g7"
+Q2QUAD = False
+W2SPLIT = ()
 GATE = 8
 CASTENG = {}
+W2ENG = {}
+SCP = ()
+QHP = ()
+QAPART = ()
 ORDER = "N"
 W2LAG = 0
 YTIE = True
-YFREE = ()
+YLAG = {}
 NEXP = 8
 PAIRS = E // 2
 LINK_SLOT = 4 * H * 4 + 64 + 2 * C * 4 + 64 + 2048
 GT_SIZE = GCH + 64 + 8 * H * 2 + 64 + 4 * C * 2
+END_OFF = 4 * LINK_SLOT + 2 * GT_SIZE
 HBTIE = ()
+LTIE = ()
+QHTIE = ()
+ENDSPLIT = False
 
 
 def tile_routed_moe_kernel(tc, xT, w1, w3, w2, gate, offs, out):
@@ -57,7 +67,6 @@ def tile_routed_moe_kernel(tc, xT, w1, w3, w2, gate, offs, out):
                 nc.gpsimd.tensor_scalar(out=dst, in0=src, scalar1=1.0, scalar2=0.0, op0=MULT, op1=ADD)
 
         offsets = lists.tile([P, E * C // 16], U16, name="offsets")
-        nc.sync.dma_start(offsets[:], offs)
 
         warm_in = keep.tile([P, 1], F32, name="warm_in")
         warm_out = keep.tile([P, 1], F32, name="warm_out")
@@ -66,17 +75,6 @@ def tile_routed_moe_kernel(tc, xT, w1, w3, w2, gate, offs, out):
 
         x_rows = xT.rearrange("(p j) n -> p j n", j=4)
         xpair = [keep.tile([P, T, 2], BF16, name="xpair%d" % u) for u in range(2)]
-        for u, t0, n, engs in XP:
-            xr = raw.tile([P, 2, n], F32, tag="raw8", name="xraw%d_%d" % (u, t0))
-            nc.sync.dma_start(xr[:], x_rows[:, 2 * u : 2 * u + 2, t0 : t0 + n])
-            w = n // len(engs)
-            for k, eng in enumerate(engs):
-                cast(
-                    eng,
-                    xpair[u][:, t0 + k * w : t0 + (k + 1) * w, :].rearrange("p (c i) e -> p c e i", i=4),
-                    xr[:, :, k * w : (k + 1) * w].rearrange("p e (c i) -> p c e i", i=4),
-                )
-
         gate_sb = keep.tile([P, E * C], F32, name="gate_sb")
         win = [keep.tile([P, T], F32, name="win%d" % nb) for nb in range(2)]
         xc = [keep.tile([P, GCH], U32, name="xc%d" % g, align_bytes=64) for g in range(NCH)]
@@ -95,9 +93,17 @@ def tile_routed_moe_kernel(tc, xT, w1, w3, w2, gate, offs, out):
             xg = work.tile([P, GCH, 4], BF16, tag="xg", name="xg%d" % g, align_bytes=64)
             words = xg[:].rearrange("p n t -> p (n t)").bitcast(U32).rearrange("p (n u) -> p n u", u=2)
             lst = offsets[:, g * (GCH // 16) : (g + 1) * (GCH // 16)]
+            if g in GPLAIN:
+                runs = keep.tile([P, 2, GCH], U32, name="runs%d" % g, align_bytes=64)
             for u in range(2):
                 window = xpair[u][:].rearrange("p n e -> p (n e)").bitcast(U32)
-                nc.vector.tensor_copy(out=words[:, :, u], in_=window.indirect(lst))
+                nc.vector.tensor_copy(out=runs[:, u, :] if g in GPLAIN else words[:, :, u], in_=window.indirect(lst))
+            if g in GPLAIN:
+                w = GCH // GPIECES
+                for k in range(GPIECES):
+                    nc.gpsimd.tensor_copy(
+                        out=words[:, k * w : (k + 1) * w, :], in_=runs[:, :, k * w : (k + 1) * w].rearrange("p u n -> p n u")
+                    )
             xgt[g] = xg
 
         def quant_x(g):
@@ -106,6 +112,7 @@ def tile_routed_moe_kernel(tc, xT, w1, w3, w2, gate, offs, out):
         rw13 = {}
         rw2 = {}
         g13 = {}
+        gql = []
         g2 = {}
         c13 = {}
         c2 = {}
@@ -132,7 +139,7 @@ def tile_routed_moe_kernel(tc, xT, w1, w3, w2, gate, offs, out):
 
         def casts13(e):
             head = 32 if e == 0 else 0
-            tail = 32 if e - 1 in HBTIE else 0
+            tail = 32 if e - 1 in HBTIE or e - 1 in QHTIE else 0
             gt = link.tile(
                 [P, head + 8 * H + tail],
                 BF16,
@@ -143,28 +150,58 @@ def tile_routed_moe_kernel(tc, xT, w1, w3, w2, gate, offs, out):
             g = gt[:, head : head + 8 * H]
             for k in range(2):
                 r = rw13[e][k]
+                eng = CASTENG.get((e, k), "S")
+                to = "p t m j" if eng == "G" else "p m j t"
                 cast(
-                    CASTENG.get((e, k), "S"),
-                    g[:, k * 4 * H : (k + 1) * 4 * H].rearrange("p (t m j) -> p m j t", t=4, j=4),
-                    r.rearrange("p j (m t) -> p m j t", t=4),
+                    eng,
+                    g[:, k * 4 * H : (k + 1) * 4 * H].rearrange("p (t m j) -> " + to, t=4, j=4),
+                    r.rearrange("p j (m t) -> " + to, t=4),
                 )
             g13[e] = g
 
         def casts2(e):
             r2 = rw2[e]
-            if e % 2 == 0:
-                g2[e // 2] = grp.tile([P, 8 * N], BF16, tag="wg2", name="g2_%d" % (e // 2), align_bytes=64)
+            if e == 4 and Q2QUAD:
+                gq = grp.tile([P, 16 * N], BF16, tag="wg4", name="g2_q", align_bytes=64, bufs=1)
+                gql.append(gq)
+                g2[2] = gq[:, 0 : 8 * N]
+                g2[3] = gq[:, 8 * N :]
+            elif e % 2 == 0 and not (Q2QUAD and e > 4):
+                g2t = grp.tile([P, 8 * N], BF16, tag="wg2", name="g2_%d" % (e // 2), align_bytes=64)
+                g2[e // 2] = g2t[:]
             o = (e % 2) * 4 * N
-            cast("G", g2[e // 2][:, o : o + 4 * N].rearrange("p (c j) -> p c j", j=4), r2[:].rearrange("p j c -> p c j"))
+            eng = W2ENG.get(e, "G")
+            if eng == "G":
+                cast("G", g2[e // 2][:, o : o + 4 * N].rearrange("p (c j) -> p c j", j=4), r2[:].rearrange("p j c -> p c j"))
+            else:
+                cast(
+                    eng,
+                    g2[e // 2][:, o : o + 4 * N].rearrange("p (c i j) -> p c j i", i=4, j=4),
+                    r2[:].rearrange("p j (c i) -> p c j i", i=4),
+                )
 
         def quant_w(e):
             c = cod.tile([P, 2 * H], U32, tag="c13", name="c13_%d" % e, align_bytes=64)
             s = cod.tile([P, 2 * H], U8, tag="s13", name="s13_%d" % e, align_bytes=64)
-            nc.vector.quantize_mx(out=c[:].bitcast(FP8X4), scales=s[:], in_=g13[e])
+            if e in QAPART:
+                for k in range(2):
+                    nc.vector.quantize_mx(
+                        out=c[:, k * H : (k + 1) * H].bitcast(FP8X4), scales=s[:, k * H : (k + 1) * H], in_=g13[e][:, 4 * k * H : 4 * (k + 1) * H]
+                    )
+            else:
+                nc.vector.quantize_mx(out=c[:].bitcast(FP8X4), scales=s[:], in_=g13[e])
             c13[e] = (c, s)
 
         def quant_w2(e):
-            if W2SPLIT:
+            if Q2QUAD and e >= 4:
+                if e == 7:
+                    c = cod.tile([P, 4 * N], U32, tag="c4", name="c2_q", align_bytes=64, bufs=1)
+                    s = cod.tile([P, 4 * N], U8, tag="s4", name="s2_q", align_bytes=64, bufs=1)
+                    nc.vector.quantize_mx(out=c[:].bitcast(FP8X4), scales=s[:], in_=gql[0][:])
+                    c2[2] = (c[:, 0 : 2 * N], s[:, 0 : 2 * N])
+                    c2[3] = (c[:, 2 * N :], s[:, 2 * N :])
+                return
+            if e // 2 in W2SPLIT:
                 if e % 2 == 0:
                     c = cod.tile([P, 2 * N], U32, tag="c2", name="c2_%d" % (e // 2), align_bytes=64)
                     s = cod.tile([P, 2 * N], U8, tag="s2", name="s2_%d" % (e // 2), align_bytes=64)
@@ -177,10 +214,13 @@ def tile_routed_moe_kernel(tc, xT, w1, w3, w2, gate, offs, out):
             elif e % 2 == 1:
                 c = cod.tile([P, 2 * N], U32, tag="c2", name="c2_%d" % (e // 2), align_bytes=64)
                 s = cod.tile([P, 2 * N], U8, tag="s2", name="s2_%d" % (e // 2), align_bytes=64)
-                nc.vector.quantize_mx(out=c[:].bitcast(FP8X4), scales=s[:], in_=g2[e // 2][:])
+                nc.vector.quantize_mx(out=c[:].bitcast(FP8X4), scales=s[:], in_=g2[e // 2])
                 c2[e // 2] = (c, s)
 
         hbt = {}
+        hpt = {}
+        ypt = {}
+        y6b = []
         yps = {}
         ysb = {}
 
@@ -201,12 +241,18 @@ def tile_routed_moe_kernel(tc, xT, w1, w3, w2, gate, offs, out):
                 )
 
         sat = {}
+        sap = {}
         bps = {}
 
         def mma(k):
             a_ps = psum.tile([P, 4, 128], F32, tag="a", name="a%d" % k, bufs=4)
             first_layer(k, 0, a_ps)
-            if k == 2 * (E - 1) and YTIE:
+            if k // 2 in LTIE:
+                q = k // 2
+                if k % 2 == 0:
+                    sap[q] = link.tile([P, 16 + 1024], F32, name="sap%d" % q, align_bytes=64, offset=((q + 1) % 4) * LINK_SLOT + 4 * H * 4)
+                sa = sap[q][:, 16 + (k % 2) * 512 : 16 + (k % 2) * 512 + 512].rearrange("p (c t) -> p c t", t=4)
+            elif k == 2 * (E - 1) + (1 if ENDSPLIT else 0) and YTIE:
                 st = link.tile([P, 16 + 512], F32, name="sa%d" % k, align_bytes=64, offset=(E % 4) * LINK_SLOT + 4 * H * 4 + 64 + 2 * C * 4)
                 sa = st[:, 16:].rearrange("p (c t) -> p c t", t=4)
             else:
@@ -222,7 +268,11 @@ def tile_routed_moe_kernel(tc, xT, w1, w3, w2, gate, offs, out):
 
         def mult(k):
             e, hf = k // 2, k % 2
-            if hf == 0:
+            if hf == 0 and e // 2 in QHP:
+                if e % 2 == 0:
+                    hpt[e // 2] = work.tile([P, 2 * C, 4], BF16, tag="hb2", name="hbp%d" % (e // 2), align_bytes=64)
+                hbt[e] = hpt[e // 2][:, (e % 2) * C : (e % 2) * C + C, :]
+            elif hf == 0:
                 if HBTIE:
                     pad = 32 if e in HBTIE else 0
                     ht = link.tile(
@@ -238,13 +288,30 @@ def tile_routed_moe_kernel(tc, xT, w1, w3, w2, gate, offs, out):
         hcs = {}
 
         def qh(e):
-            hc = work.tile([P, C], U32, tag="hc", name="hc%d" % e, align_bytes=64)
-            if YTIE:
+            if e // 2 in QHP:
+                if e % 2 == 1:
+                    hc = work.tile([P, 2 * C], U32, tag="hc2", name="hcp%d" % (e // 2), align_bytes=64)
+                    hs = work.tile([P, 2 * C], U8, tag="hs2", name="hsp%d" % (e // 2), align_bytes=64)
+                    nc.vector.quantize_mx(out=hc[:].bitcast(FP8X4), scales=hs[:], in_=hpt[e // 2][:].rearrange("p c t -> p (c t)"))
+                    for k in range(2):
+                        hcs[e - 1 + k] = (hc[:, k * C : (k + 1) * C], hs[:, k * C : (k + 1) * C])
+                return
+            if ENDSPLIT and e == E - 1:
+                hct = link.tile([P, C + 16], U32, name="hc%d" % e, align_bytes=64, offset=END_OFF)
+                hc = hct[:, 0:C]
+            else:
+                hct = work.tile([P, C], U32, tag="hc", name="hc%d" % e, align_bytes=64)
+                hc = hct[:]
+            if e in QHTIE:
+                hst = link.tile(
+                    [P, 64 + C], U8, name="hs%d" % e, align_bytes=64, offset=4 * LINK_SLOT + ((e + 1) % 2) * GT_SIZE + GCH + 64 + 8 * H * 2
+                )
+            elif YTIE:
                 hst = link.tile([P, 64 + C], U8, name="hs%d" % e, align_bytes=64, offset=(e % 4) * LINK_SLOT + 4 * H * 4 + 64 + 2 * C * 4)
             else:
                 hst = work.tile([P, 64 + C], U8, tag="hs", name="hs%d" % e, align_bytes=64)
             hs = hst[:, 64:]
-            nc.vector.quantize_mx(out=hc[:].bitcast(FP8X4), scales=hs, in_=hbt[e].rearrange("p c t -> p (c t)"))
+            nc.vector.quantize_mx(out=hc.bitcast(FP8X4), scales=hs, in_=hbt[e].rearrange("p c t -> p (c t)"))
             hcs[e] = (hc, hs)
 
         def mm2(e):
@@ -257,7 +324,7 @@ def tile_routed_moe_kernel(tc, xT, w1, w3, w2, gate, offs, out):
                     out=y_ps[:, nb, :],
                     lhsT=c[:, col : col + 128].bitcast(FP8X4),
                     lhsT_scale=s[:, col : col + 128],
-                    rhs=hc[:].bitcast(FP8X4),
+                    rhs=hc.bitcast(FP8X4),
                     rhs_scale=hs,
                     start=True,
                     stop=True,
@@ -265,23 +332,66 @@ def tile_routed_moe_kernel(tc, xT, w1, w3, w2, gate, offs, out):
             yps[e] = y_ps
 
         def evac(e):
-            if e in YFREE:
+            if e // 2 in SCP:
+                if e % 2 == 0:
+                    ypt[e // 2] = work.tile([P, 2, 2 * C], F32, tag="yp", name="yp%d" % (e // 2), align_bytes=64)
+                y = ypt[e // 2][:, :, (e % 2) * C : (e % 2) * C + C]
+                nc.scalar.copy(out=y, in_=yps[e][:])
+                return
+            lag = YLAG.get(e, 2)
+            if lag == 0:
                 yt = keep.tile([P, 16 + 2 * C + 16], F32, name="ysb%d" % e, align_bytes=64)
             else:
                 yt = link.tile(
-                    [P, 16 + 2 * C + 16], F32, name="ysb%d" % e, align_bytes=64, offset=((e + 2) % 4) * LINK_SLOT + 4 * H * 4
+                    [P, 16 + 2 * C + 16], F32, name="ysb%d" % e, align_bytes=64, offset=((e + lag) % 4) * LINK_SLOT + 4 * H * 4
                 )
             y = yt[:, 16 : 16 + 2 * C].rearrange("p (n c) -> p n c", n=2)
-            nc.scalar.copy(out=y, in_=yps[e][:])
             ysb[e] = y
+            if ENDSPLIT and e >= E - 2:
+                nc.scalar.copy(out=y[:, 0, :], in_=yps[e][:, 0, :])
+                if e == E - 1:
+                    y6 = link.tile([P, 16 + C], F32, name="ysb6b", align_bytes=64, offset=END_OFF + 4 * C)
+                    nc.scalar.copy(out=y6[:, 16:], in_=yps[e - 1][:, 1, :])
+                    y6b.append(y6)
+                    nc.scalar.copy(out=y[:, 1, :], in_=yps[e][:, 1, :])
+            else:
+                nc.scalar.copy(out=y, in_=yps[e][:])
 
         def scatter(e, nb):
+            if e // 2 in SCP:
+                if e % 2 == 1:
+                    q = e // 2
+                    nc.vector.tensor_tensor(
+                        out=win[nb][:].indirect(offsets[:, q * (C // 8) : (q + 1) * (C // 8)]),
+                        in0=ypt[q][:, nb, :],
+                        in1=gate_sb[:, 2 * q * C : 2 * (q + 1) * C],
+                        op=MULT,
+                    )
+                return
             lst = offsets[:, e * (C // 16) : (e + 1) * (C // 16)]
             nc.vector.tensor_tensor(
-                out=win[nb][:].indirect(lst), in0=ysb[e][:, nb, :], in1=gate_sb[:, e * C : (e + 1) * C], op=MULT
+                out=win[nb][:].indirect(lst),
+                in0=y6b[0][:, 16:] if y6b and e == E - 2 and nb == 1 else ysb[e][:, nb, :],
+                in1=gate_sb[:, e * C : (e + 1) * C],
+                op=MULT,
             )
 
-        loaders = {"a": loada, "b": loadb, "c": load2, "g": loadg}
+        def loadx(i):
+            u, t0, n, engs = XP[i]
+            xr = raw.tile([P, 2, n], F32, tag="raw8" if n > 512 else "raw4", name="xraw%d_%d" % (u, t0), bufs=4)
+            nc.sync.dma_start(xr[:], x_rows[:, 2 * u : 2 * u + 2, t0 : t0 + n])
+            w = n // len(engs)
+            for k, eng in enumerate(engs):
+                cast(
+                    eng,
+                    xpair[u][:, t0 + k * w : t0 + (k + 1) * w, :].rearrange("p (c i) e -> p c e i", i=4),
+                    xr[:, :, k * w : (k + 1) * w].rearrange("p e (c i) -> p c e i", i=4),
+                )
+
+        def loado(i):
+            nc.sync.dma_start(offsets[:], offs)
+
+        loaders = {"o": loado, "x": loadx, "a": loada, "b": loadb, "c": load2, "g": loadg}
         loaded = set()
 
         def load(kind, n):
@@ -292,9 +402,17 @@ def tile_routed_moe_kernel(tc, xT, w1, w3, w2, gate, offs, out):
         if NEXP < E:
             for nb in range(2):
                 nc.vector.memset(win[nb][:], 0.0)
-        for tok in LOADS.split(" "):
-            if int(tok[1:]) < NEXP:
-                load(tok[0], int(tok[1:]))
+        queue = [t for t in SEQ.split(" ") if (t[0] in "xo" or int(t[1:]) < NEXP) and (t[0] != "g" or int(t[1:]) < GATE)]
+
+        def load_to(last):
+            while queue:
+                t = queue[0]
+                queue.remove(t)
+                load(t[0], int(t[1:]))
+                if t == last:
+                    break
+
+        load_to("b%d" % min(3, NEXP - 1))
         gather(0)
         quant_x(0)
         gather(1)
@@ -316,22 +434,30 @@ def tile_routed_moe_kernel(tc, xT, w1, w3, w2, gate, offs, out):
         mma(0)
         mma(1)
         for e in range(NEXP):
-            for tok in LATE.split(" "):
-                n = e + 4 - int(tok[1:])
-                if n < NEXP and (tok[0], n) not in loaded:
-                    load(tok[0], n)
+            if e + 4 < NEXP:
+                load_to("b%d" % (e + 4))
+            elif e + 4 == NEXP:
+                load_to("")
             if e + 1 < NEXP:
                 mma(2 * e + 2)
                 mma(2 * e + 3)
             mmb(2 * e)
             mmb(2 * e + 1)
             mult(2 * e)
-            if e >= 1:
+            if e >= 1 and not ((e - 1) // 2 in QHP and e % 2 == 1):
+                if e % 2 == 0 and (e - 1) // 2 in QHP:
+                    mm2(e - 2)
+                    evac(e - 2)
                 mm2(e - 1)
                 evac(e - 1)
-            if e >= 2:
+            if e >= 2 and not (e - 2) // 2 in QHP:
                 scatter(e - 2, 0)
                 scatter(e - 2, 1)
+            if e >= 3 and (e - 3) // 2 in QHP:
+                scatter(e - 3, 0)
+                scatter(e - 3, 1)
+                if e % 2 == 1:
+                    pass
             mult(2 * e + 1)
             qh(e)
             if e + 2 < NEXP:
@@ -341,9 +467,15 @@ def tile_routed_moe_kernel(tc, xT, w1, w3, w2, gate, offs, out):
                 quant_w2(e + 2)
         mm2(NEXP - 1)
         evac(NEXP - 1)
+        if (NEXP - 3) // 2 in QHP:
+            scatter(NEXP - 3, 0)
+            scatter(NEXP - 3, 1)
         if NEXP > 1:
             scatter(NEXP - 2, 0)
-            scatter(NEXP - 2, 1)
+            if not ENDSPLIT:
+                scatter(NEXP - 2, 1)
         for nb in range(2):
+            if ENDSPLIT and nb == 1:
+                scatter(NEXP - 2, 1)
             scatter(NEXP - 1, nb)
             nc.sync.dma_start(out[nb * P : (nb + 1) * P, :], win[nb][:])

@@ -21,13 +21,13 @@ GCH = 1024
 GPLAIN = ()
 GPIECES = 4
 NCH = E * C // GCH
-XP = ((0, 0, 1024, "S"), (0, 1024, 512, "V"), (0, 1536, 256, "V"), (0, 1792, 256, "V"), (1, 0, 1024, "S"), (1, 1024, 512, "G"), (1, 1536, 512, "SG"))
-SEQ = "x0 x1 x2 x3 o0 x4 x5 x6 a0 b0 a1 c0 g0 b1 a2 c1 g1 b2 a3 c2 g2 b3 a4 c3 g3 b4 a5 c4 g4 b5 a6 c5 g5 b6 a7 c6 g6 b7 c7 g7"
+XP = ((0, 0, 1024, "S"), (0, 1024, 512, "V"), (0, 1536, 256, "V"), (0, 1792, 256, "V"), (1, 0, 1024, "S"), (1, 1024, 1024, "SV"))
+SEQ = "x0 x1 x2 x3 o0 x4 x5 a0 b0 a1 b1 c0 a2 c1 g0 b2 a3 c2 g1 b3 a4 c3 g2 b4 a5 c4 g3 b5 a6 c5 g4 b6 a7 c6 g5 b7 c7 g6 g7"
 Q2QUAD = False
 W2SPLIT = ()
 GATE = 8
 CASTENG = {}
-W2ENG = {}
+W2ENG = {0: "V", 1: "V"}
 SCP = ()
 QHP = ()
 QAPART = ()
@@ -41,7 +41,7 @@ LINK_SLOT = 4 * H * 4 + 64 + 2 * C * 4 + 64 + 2048
 GT_SIZE = GCH + 64 + 8 * H * 2 + 64 + 4 * C * 2
 END_OFF = 4 * LINK_SLOT + 2 * GT_SIZE
 HBTIE = ()
-LTIE = ()
+LTIE = (0,)
 QHTIE = ()
 ENDSPLIT = False
 

from contextlib import ExitStack

import concourse.mybir as mybir

K, T, E, C, H, N = 512, 2048, 8, 256, 512, 256
FLOPS = 2 * E * C * (2 * K * H + H * N)
BYTES = 4 * (K * T + 2 * E * K * H + E * H * N + E * C + N * T) + 2 * 128 * 128

F32 = mybir.dt.float32
BF16 = mybir.dt.bfloat16
U32 = mybir.dt.uint32
U16 = mybir.dt.uint16
U8 = mybir.dt.uint8
FP8X4 = mybir.dt.float8_e4m3fn_x4
MULT = mybir.AluOpType.mult
ADD = mybir.AluOpType.add
SILU = mybir.ActivationFunctionType.Silu

P = 128
GCH = 1024
GPLAIN = ()
GPIECES = 4
NCH = E * C // GCH
XP = ((0, 0, 1024, "S"), (0, 1024, 512, "V"), (0, 1536, 256, "V"), (0, 1792, 256, "V"), (1, 0, 1024, "S"), (1, 1024, 1024, "SV"))
SEQ = "x0 x1 x2 x3 o0 x4 x5 a0 b0 a1 b1 c0 a2 c1 g0 b2 a3 c2 g1 b3 a4 c3 g2 b4 a5 c4 g3 b5 a6 c5 g4 b6 a7 c6 g5 b7 c7 g6 g7"
Q2QUAD = False
W2SPLIT = ()
GATE = 8
CASTENG = {}
W2ENG = {0: "V", 1: "V"}
SCP = ()
QHP = ()
QAPART = ()
ORDER = "N"
W2LAG = 0
YTIE = True
YLAG = {}
NEXP = 8
PAIRS = E // 2
LINK_SLOT = 4 * H * 4 + 64 + 2 * C * 4 + 64 + 2048
GT_SIZE = GCH + 64 + 8 * H * 2 + 64 + 4 * C * 2
END_OFF = 4 * LINK_SLOT + 2 * GT_SIZE
HBTIE = ()
LTIE = (0,)
QHTIE = ()
ENDSPLIT = False


def tile_routed_moe_kernel(tc, xT, w1, w3, w2, gate, offs, out):
    nc = tc.nc
    with ExitStack() as ctx:
        lists = ctx.enter_context(tc.tile_pool(name="lists", bufs=1))
        keep = ctx.enter_context(tc.tile_pool(name="keep", bufs=1))
        raw = ctx.enter_context(tc.tile_pool(name="raw", bufs=4))
        link = ctx.enter_context(tc.tile_pool(name="link", bufs=1))
        grp = ctx.enter_context(tc.tile_pool(name="grp", bufs=2))
        cod = ctx.enter_context(tc.tile_pool(name="cod", bufs=2))
        work = ctx.enter_context(tc.tile_pool(name="work", bufs=2))
        psum = ctx.enter_context(tc.psum_pool(name="psum", bufs=3))

        def cast(eng, dst, src):
            if eng == "V":
                nc.vector.tensor_copy(out=dst, in_=src)
            elif eng == "S":
                nc.scalar.copy(out=dst, in_=src)
            else:
                nc.gpsimd.tensor_scalar(out=dst, in0=src, scalar1=1.0, scalar2=0.0, op0=MULT, op1=ADD)

        offsets = lists.tile([P, E * C // 16], U16, name="offsets")

        warm_in = keep.tile([P, 1], F32, name="warm_in")
        warm_out = keep.tile([P, 1], F32, name="warm_out")
        nc.vector.memset(warm_in[:], 0.0)
        nc.scalar.activation(out=warm_out[:], in_=warm_in[:], func=SILU)

        x_rows = xT.rearrange("(p j) n -> p j n", j=4)
        xpair = [keep.tile([P, T, 2], BF16, name="xpair%d" % u) for u in range(2)]
        gate_sb = keep.tile([P, E * C], F32, name="gate_sb")
        win = [keep.tile([P, T], F32, name="win%d" % nb) for nb in range(2)]
        xc = [keep.tile([P, GCH], U32, name="xc%d" % g, align_bytes=64) for g in range(NCH)]
        xs = []
        for g in range(NCH):
            if g == NCH - 1:
                xs1 = link.tile([P, GCH + 64], U8, name="xs1", align_bytes=64, offset=4 * LINK_SLOT)
                xs.append(xs1[:, 0:GCH])
            else:
                xs0 = keep.tile([P, GCH], U8, name="xs%d" % g, align_bytes=64)
                xs.append(xs0[:])

        xgt = {}

        def gather(g):
            xg = work.tile([P, GCH, 4], BF16, tag="xg", name="xg%d" % g, align_bytes=64)
            words = xg[:].rearrange("p n t -> p (n t)").bitcast(U32).rearrange("p (n u) -> p n u", u=2)
            lst = offsets[:, g * (GCH // 16) : (g + 1) * (GCH // 16)]
            if g in GPLAIN:
                runs = keep.tile([P, 2, GCH], U32, name="runs%d" % g, align_bytes=64)
            for u in range(2):
                window = xpair[u][:].rearrange("p n e -> p (n e)").bitcast(U32)
                nc.vector.tensor_copy(out=runs[:, u, :] if g in GPLAIN else words[:, :, u], in_=window.indirect(lst))
            if g in GPLAIN:
                w = GCH // GPIECES
                for k in range(GPIECES):
                    nc.gpsimd.tensor_copy(
                        out=words[:, k * w : (k + 1) * w, :], in_=runs[:, :, k * w : (k + 1) * w].rearrange("p u n -> p n u")
                    )
            xgt[g] = xg

        def quant_x(g):
            nc.vector.quantize_mx(out=xc[g][:].bitcast(FP8X4), scales=xs[g], in_=xgt[g][:].rearrange("p n t -> p (n t)"))

        rw13 = {}
        rw2 = {}
        g13 = {}
        gql = []
        g2 = {}
        c13 = {}
        c2 = {}

        def loadg(k):
            n = E * C // GATE
            nc.sync.dma_start(gate_sb[:, k * n : (k + 1) * n], gate[0:P, k * n : (k + 1) * n])

        def loada(e):
            r1t = raw.tile([P, 4, H], F32, tag="raw8", name="r1_%d" % e)
            nc.sync.dma_start(r1t[:], w1[e].rearrange("(p j) c -> p j c", j=4))
            rw13[e] = [r1t[:], None]

        def loadb(e):
            r3t = link.tile([P, 4 * H + 16], F32, name="r3_%d" % e, align_bytes=64, offset=(e % 4) * LINK_SLOT)
            r3 = r3t[:, 0 : 4 * H].rearrange("p (j c) -> p j c", j=4)
            nc.sync.dma_start(r3, w3[e].rearrange("(p j) c -> p j c", j=4))
            rw13[e][1] = r3

        def load2(e):
            r2 = raw.tile([P, 4, N], F32, tag="raw4", name="r2_%d" % e, bufs=4)
            nc.sync.dma_start(r2[:], w2[e].rearrange("(p j) c -> p j c", j=4))
            rw2[e] = r2

        def casts13(e):
            head = 32 if e == 0 else 0
            tail = 32 if e - 1 in HBTIE or e - 1 in QHTIE else 0
            gt = link.tile(
                [P, head + 8 * H + tail],
                BF16,
                name="g13_%d" % e,
                align_bytes=64,
                offset=4 * LINK_SLOT + (e % 2) * GT_SIZE + GCH + 64 - 2 * head,
            )
            g = gt[:, head : head + 8 * H]
            for k in range(2):
                r = rw13[e][k]
                eng = CASTENG.get((e, k), "S")
                to = "p t m j" if eng == "G" else "p m j t"
                cast(
                    eng,
                    g[:, k * 4 * H : (k + 1) * 4 * H].rearrange("p (t m j) -> " + to, t=4, j=4),
                    r.rearrange("p j (m t) -> " + to, t=4),
                )
            g13[e] = g

        def casts2(e):
            r2 = rw2[e]
            if e == 4 and Q2QUAD:
                gq = grp.tile([P, 16 * N], BF16, tag="wg4", name="g2_q", align_bytes=64, bufs=1)
                gql.append(gq)
                g2[2] = gq[:, 0 : 8 * N]
                g2[3] = gq[:, 8 * N :]
            elif e % 2 == 0 and not (Q2QUAD and e > 4):
                g2t = grp.tile([P, 8 * N], BF16, tag="wg2", name="g2_%d" % (e // 2), align_bytes=64)
                g2[e // 2] = g2t[:]
            o = (e % 2) * 4 * N
            eng = W2ENG.get(e, "G")
            if eng == "G":
                cast("G", g2[e // 2][:, o : o + 4 * N].rearrange("p (c j) -> p c j", j=4), r2[:].rearrange("p j c -> p c j"))
            else:
                cast(
                    eng,
                    g2[e // 2][:, o : o + 4 * N].rearrange("p (c i j) -> p c j i", i=4, j=4),
                    r2[:].rearrange("p j (c i) -> p c j i", i=4),
                )

        def quant_w(e):
            c = cod.tile([P, 2 * H], U32, tag="c13", name="c13_%d" % e, align_bytes=64)
            s = cod.tile([P, 2 * H], U8, tag="s13", name="s13_%d" % e, align_bytes=64)
            if e in QAPART:
                for k in range(2):
                    nc.vector.quantize_mx(
                        out=c[:, k * H : (k + 1) * H].bitcast(FP8X4), scales=s[:, k * H : (k + 1) * H], in_=g13[e][:, 4 * k * H : 4 * (k + 1) * H]
                    )
            else:
                nc.vector.quantize_mx(out=c[:].bitcast(FP8X4), scales=s[:], in_=g13[e])
            c13[e] = (c, s)

        def quant_w2(e):
            if Q2QUAD and e >= 4:
                if e == 7:
                    c = cod.tile([P, 4 * N], U32, tag="c4", name="c2_q", align_bytes=64, bufs=1)
                    s = cod.tile([P, 4 * N], U8, tag="s4", name="s2_q", align_bytes=64, bufs=1)
                    nc.vector.quantize_mx(out=c[:].bitcast(FP8X4), scales=s[:], in_=gql[0][:])
                    c2[2] = (c[:, 0 : 2 * N], s[:, 0 : 2 * N])
                    c2[3] = (c[:, 2 * N :], s[:, 2 * N :])
                return
            if e // 2 in W2SPLIT:
                if e % 2 == 0:
                    c = cod.tile([P, 2 * N], U32, tag="c2", name="c2_%d" % (e // 2), align_bytes=64)
                    s = cod.tile([P, 2 * N], U8, tag="s2", name="s2_%d" % (e // 2), align_bytes=64)
                    c2[e // 2] = (c, s)
                c, s = c2[e // 2]
                o = (e % 2) * N
                nc.vector.quantize_mx(
                    out=c[:, o : o + N].bitcast(FP8X4), scales=s[:, o : o + N], in_=g2[e // 2][:, 4 * o : 4 * o + 4 * N]
                )
            elif e % 2 == 1:
                c = cod.tile([P, 2 * N], U32, tag="c2", name="c2_%d" % (e // 2), align_bytes=64)
                s = cod.tile([P, 2 * N], U8, tag="s2", name="s2_%d" % (e // 2), align_bytes=64)
                nc.vector.quantize_mx(out=c[:].bitcast(FP8X4), scales=s[:], in_=g2[e // 2])
                c2[e // 2] = (c, s)

        hbt = {}
        hpt = {}
        ypt = {}
        y6b = []
        yps = {}
        ysb = {}

        def first_layer(k, m, ps):
            e = k // 2
            c, s = c13[e]
            g, o = (k * 128) // GCH, (k * 128) % GCH
            for t in range(4):
                col = m * H + 128 * t
                nc.tensor.matmul_mx(
                    out=ps[:, t, :],
                    lhsT=c[:, col : col + 128].bitcast(FP8X4),
                    lhsT_scale=s[:, col : col + 128],
                    rhs=xc[g][:, o : o + 128].bitcast(FP8X4),
                    rhs_scale=xs[g][:, o : o + 128],
                    start=True,
                    stop=True,
                )

        sat = {}
        sap = {}
        bps = {}

        def mma(k):
            a_ps = psum.tile([P, 4, 128], F32, tag="a", name="a%d" % k, bufs=4)
            first_layer(k, 0, a_ps)
            if k // 2 in LTIE:
                q = k // 2
                if k % 2 == 0:
                    sap[q] = link.tile([P, 16 + 1024], F32, name="sap%d" % q, align_bytes=64, offset=((q + 1) % 4) * LINK_SLOT + 4 * H * 4)
                sa = sap[q][:, 16 + (k % 2) * 512 : 16 + (k % 2) * 512 + 512].rearrange("p (c t) -> p c t", t=4)
            elif k == 2 * (E - 1) + (1 if ENDSPLIT else 0) and YTIE:
                st = link.tile([P, 16 + 512], F32, name="sa%d" % k, align_bytes=64, offset=(E % 4) * LINK_SLOT + 4 * H * 4 + 64 + 2 * C * 4)
                sa = st[:, 16:].rearrange("p (c t) -> p c t", t=4)
            else:
                st = work.tile([P, 128, 4], F32, tag="sa", name="sa%d" % k, bufs=6)
                sa = st[:]
            nc.scalar.activation(out=sa, in_=a_ps[:].rearrange("p t c -> p c t"), func=SILU)
            sat[k] = sa

        def mmb(k):
            b_ps = psum.tile([P, 4, 128], F32, tag="by", name="b%d" % k, bufs=4)
            first_layer(k, 1, b_ps)
            bps[k] = b_ps

        def mult(k):
            e, hf = k // 2, k % 2
            if hf == 0 and e // 2 in QHP:
                if e % 2 == 0:
                    hpt[e // 2] = work.tile([P, 2 * C, 4], BF16, tag="hb2", name="hbp%d" % (e // 2), align_bytes=64)
                hbt[e] = hpt[e // 2][:, (e % 2) * C : (e % 2) * C + C, :]
            elif hf == 0:
                if HBTIE:
                    pad = 32 if e in HBTIE else 0
                    ht = link.tile(
                        [P, pad + 4 * C], BF16, name="hb%d" % e, align_bytes=64, offset=4 * LINK_SLOT + ((e + 1) % 2) * GT_SIZE + GCH + 128 + 8 * H * 2 - 2 * pad
                    )
                    hbt[e] = ht[:, pad:].rearrange("p (c t) -> p c t", t=4)
                else:
                    hbt[e] = work.tile([P, C, 4], BF16, tag="hb", name="hb%d" % e, align_bytes=64)[:]
            nc.vector.tensor_tensor(
                out=hbt[e][:, hf * 128 : hf * 128 + 128, :], in0=sat[k], in1=bps[k][:].rearrange("p t c -> p c t"), op=MULT
            )

        hcs = {}

        def qh(e):
            if e // 2 in QHP:
                if e % 2 == 1:
                    hc = work.tile([P, 2 * C], U32, tag="hc2", name="hcp%d" % (e // 2), align_bytes=64)
                    hs = work.tile([P, 2 * C], U8, tag="hs2", name="hsp%d" % (e // 2), align_bytes=64)
                    nc.vector.quantize_mx(out=hc[:].bitcast(FP8X4), scales=hs[:], in_=hpt[e // 2][:].rearrange("p c t -> p (c t)"))
                    for k in range(2):
                        hcs[e - 1 + k] = (hc[:, k * C : (k + 1) * C], hs[:, k * C : (k + 1) * C])
                return
            if ENDSPLIT and e == E - 1:
                hct = link.tile([P, C + 16], U32, name="hc%d" % e, align_bytes=64, offset=END_OFF)
                hc = hct[:, 0:C]
            else:
                hct = work.tile([P, C], U32, tag="hc", name="hc%d" % e, align_bytes=64)
                hc = hct[:]
            if e in QHTIE:
                hst = link.tile(
                    [P, 64 + C], U8, name="hs%d" % e, align_bytes=64, offset=4 * LINK_SLOT + ((e + 1) % 2) * GT_SIZE + GCH + 64 + 8 * H * 2
                )
            elif YTIE:
                hst = link.tile([P, 64 + C], U8, name="hs%d" % e, align_bytes=64, offset=(e % 4) * LINK_SLOT + 4 * H * 4 + 64 + 2 * C * 4)
            else:
                hst = work.tile([P, 64 + C], U8, tag="hs", name="hs%d" % e, align_bytes=64)
            hs = hst[:, 64:]
            nc.vector.quantize_mx(out=hc.bitcast(FP8X4), scales=hs, in_=hbt[e].rearrange("p c t -> p (c t)"))
            hcs[e] = (hc, hs)

        def mm2(e):
            c, s = c2[e // 2]
            hc, hs = hcs[e]
            y_ps = psum.tile([P, 2, C], F32, tag="by", name="y%d" % e, bufs=4)
            for nb in range(2):
                col = (e % 2) * N + nb * 128
                nc.tensor.matmul_mx(
                    out=y_ps[:, nb, :],
                    lhsT=c[:, col : col + 128].bitcast(FP8X4),
                    lhsT_scale=s[:, col : col + 128],
                    rhs=hc.bitcast(FP8X4),
                    rhs_scale=hs,
                    start=True,
                    stop=True,
                )
            yps[e] = y_ps

        def evac(e):
            if e // 2 in SCP:
                if e % 2 == 0:
                    ypt[e // 2] = work.tile([P, 2, 2 * C], F32, tag="yp", name="yp%d" % (e // 2), align_bytes=64)
                y = ypt[e // 2][:, :, (e % 2) * C : (e % 2) * C + C]
                nc.scalar.copy(out=y, in_=yps[e][:])
                return
            lag = YLAG.get(e, 2)
            if lag == 0:
                yt = keep.tile([P, 16 + 2 * C + 16], F32, name="ysb%d" % e, align_bytes=64)
            else:
                yt = link.tile(
                    [P, 16 + 2 * C + 16], F32, name="ysb%d" % e, align_bytes=64, offset=((e + lag) % 4) * LINK_SLOT + 4 * H * 4
                )
            y = yt[:, 16 : 16 + 2 * C].rearrange("p (n c) -> p n c", n=2)
            ysb[e] = y
            if ENDSPLIT and e >= E - 2:
                nc.scalar.copy(out=y[:, 0, :], in_=yps[e][:, 0, :])
                if e == E - 1:
                    y6 = link.tile([P, 16 + C], F32, name="ysb6b", align_bytes=64, offset=END_OFF + 4 * C)
                    nc.scalar.copy(out=y6[:, 16:], in_=yps[e - 1][:, 1, :])
                    y6b.append(y6)
                    nc.scalar.copy(out=y[:, 1, :], in_=yps[e][:, 1, :])
            else:
                nc.scalar.copy(out=y, in_=yps[e][:])

        def scatter(e, nb):
            if e // 2 in SCP:
                if e % 2 == 1:
                    q = e // 2
                    nc.vector.tensor_tensor(
                        out=win[nb][:].indirect(offsets[:, q * (C // 8) : (q + 1) * (C // 8)]),
                        in0=ypt[q][:, nb, :],
                        in1=gate_sb[:, 2 * q * C : 2 * (q + 1) * C],
                        op=MULT,
                    )
                return
            lst = offsets[:, e * (C // 16) : (e + 1) * (C // 16)]
            nc.vector.tensor_tensor(
                out=win[nb][:].indirect(lst),
                in0=y6b[0][:, 16:] if y6b and e == E - 2 and nb == 1 else ysb[e][:, nb, :],
                in1=gate_sb[:, e * C : (e + 1) * C],
                op=MULT,
            )

        def loadx(i):
            u, t0, n, engs = XP[i]
            xr = raw.tile([P, 2, n], F32, tag="raw8" if n > 512 else "raw4", name="xraw%d_%d" % (u, t0), bufs=4)
            nc.sync.dma_start(xr[:], x_rows[:, 2 * u : 2 * u + 2, t0 : t0 + n])
            w = n // len(engs)
            for k, eng in enumerate(engs):
                cast(
                    eng,
                    xpair[u][:, t0 + k * w : t0 + (k + 1) * w, :].rearrange("p (c i) e -> p c e i", i=4),
                    xr[:, :, k * w : (k + 1) * w].rearrange("p e (c i) -> p c e i", i=4),
                )

        def loado(i):
            nc.sync.dma_start(offsets[:], offs)

        loaders = {"o": loado, "x": loadx, "a": loada, "b": loadb, "c": load2, "g": loadg}
        loaded = set()

        def load(kind, n):
            if kind != "g" or n < GATE:
                loaders[kind](n)
            loaded.add((kind, n))

        if NEXP < E:
            for nb in range(2):
                nc.vector.memset(win[nb][:], 0.0)
        queue = [t for t in SEQ.split(" ") if (t[0] in "xo" or int(t[1:]) < NEXP) and (t[0] != "g" or int(t[1:]) < GATE)]

        def load_to(last):
            while queue:
                t = queue[0]
                queue.remove(t)
                load(t[0], int(t[1:]))
                if t == last:
                    break

        load_to("b%d" % min(3, NEXP - 1))
        gather(0)
        quant_x(0)
        gather(1)
        if NCH == 4:
            quant_x(1)
            gather(2)
            quant_x(2)
            gather(3)
        casts13(0)
        casts2(0)
        quant_w(0)
        quant_w2(0)
        quant_x(NCH - 1)
        if NEXP > 1:
            casts13(1)
            casts2(1)
            quant_w(1)
            quant_w2(1)
        mma(0)
        mma(1)
        for e in range(NEXP):
            if e + 4 < NEXP:
                load_to("b%d" % (e + 4))
            elif e + 4 == NEXP:
                load_to("")
            if e + 1 < NEXP:
                mma(2 * e + 2)
                mma(2 * e + 3)
            mmb(2 * e)
            mmb(2 * e + 1)
            mult(2 * e)
            if e >= 1 and not ((e - 1) // 2 in QHP and e % 2 == 1):
                if e % 2 == 0 and (e - 1) // 2 in QHP:
                    mm2(e - 2)
                    evac(e - 2)
                mm2(e - 1)
                evac(e - 1)
            if e >= 2 and not (e - 2) // 2 in QHP:
                scatter(e - 2, 0)
                scatter(e - 2, 1)
            if e >= 3 and (e - 3) // 2 in QHP:
                scatter(e - 3, 0)
                scatter(e - 3, 1)
                if e % 2 == 1:
                    pass
            mult(2 * e + 1)
            qh(e)
            if e + 2 < NEXP:
                casts13(e + 2)
                casts2(e + 2)
                quant_w(e + 2)
                quant_w2(e + 2)
        mm2(NEXP - 1)
        evac(NEXP - 1)
        if (NEXP - 3) // 2 in QHP:
            scatter(NEXP - 3, 0)
            scatter(NEXP - 3, 1)
        if NEXP > 1:
            scatter(NEXP - 2, 0)
            if not ENDSPLIT:
                scatter(NEXP - 2, 1)
        for nb in range(2):
            if ENDSPLIT and nb == 1:
                scatter(NEXP - 2, 1)
            scatter(NEXP - 1, nb)
            nc.sync.dma_start(out[nb * P : (nb + 1) * P, :], win[nb][:])
